import numpy as np
import ml_dtypes


def mxq(x, axis, fmt="e4m3"):
    dtype, down = {"e4m3": (ml_dtypes.float8_e4m3fn, 7), "e5m2": (ml_dtypes.float8_e5m2, 14)}[fmt]
    v = np.moveaxis(np.asarray(x, np.float32).astype(ml_dtypes.bfloat16).astype(np.float64), axis, -1)
    blocks = v.reshape(v.shape[:-1] + (-1, 32))
    amax = np.abs(blocks).max(-1, keepdims=True)
    byte = np.maximum(np.where(amax > 0, np.frexp(amax)[1] - 1 + 127, 0) - down, 1)
    scale = np.exp2(byte - 127.0)
    codes = (blocks / scale).astype(np.float32).astype(dtype).astype(np.float64)
    return np.moveaxis((codes * scale).reshape(v.shape), -1, axis)


WIDE = False


def mx_kscale(k):
    if not WIDE:
        return np.ones(k)
    levels = np.array([10, -10, 5, -5, 0])
    if k % 512:
        return np.exp2(np.random.permutation(np.resize(levels, k // 32))).repeat(32)
    a = np.empty((k // 512, 16))
    for p in range(k // 512):
        a[p, :8] = np.random.permutation(np.resize(levels, 8))
        for g in range(8):
            far = levels[np.abs(levels - a[p, g]) >= 10]
            a[p, g + 8] = far[np.random.randint(len(far))]
    return np.exp2(a.ravel()).repeat(32)


BF16 = ml_dtypes.bfloat16


def bf(x):
    return np.asarray(x, np.float32).astype(BF16)


def f64(x):
    return np.asarray(x).astype(np.float64)


E2M1 = np.array([0.0, 0.5, 1.0, 1.5, 2.0, 3.0, 4.0, 6.0, -0.0, -0.5, -1.0, -1.5, -2.0, -3.0, -4.0, -6.0])


def pack_weight(w, fmt):
    k, n = w.shape
    w = f64(bf(w)).reshape(k // 32, 32, n)
    amax = np.abs(w).max(1)
    if fmt == "e4m3":
        byte = np.frexp(amax)[1] - 1 + 127 - 7
    else:
        mant, ex = np.frexp(amax / 6.0)
        byte = np.where(mant > 0.5, ex, ex - 1) + 127
    byte = np.clip(np.where(amax > 0, byte, 1), 1, 254)
    scaled = (w * np.exp2(127.0 - byte)[:, None, :]).reshape(k, n).astype(np.float32)
    by_word = np.ascontiguousarray(scaled.reshape(k // 512, 128, 4, n).transpose(0, 1, 3, 2))
    if fmt == "e4m3":
        words = by_word.astype(ml_dtypes.float8_e4m3fn).view(np.uint8)
    else:
        c = by_word.astype(ml_dtypes.float4_e2m1fn).view(np.uint8) & 0xF
        words = c[..., 0::2] | (c[..., 1::2] << 4)
    return np.ascontiguousarray(words), np.ascontiguousarray(byte.astype(np.uint8).reshape(k // 512, 16, n))


def unpack_weight(words, scales, fmt):
    g, p, n, _ = words.shape
    if fmt == "e4m3":
        vals = np.ascontiguousarray(words).view(ml_dtypes.float8_e4m3fn).astype(np.float64)
    else:
        nib = np.empty((g, p, n, 4), np.uint8)
        nib[..., 0::2] = words & 0xF
        nib[..., 1::2] = words >> 4
        vals = E2M1[nib]
    vals = vals * np.repeat(np.exp2(scales.astype(np.float64) - 127.0), 8, axis=1)[..., None]
    return vals.transpose(0, 1, 3, 2).reshape(g * 512, n)
def pack4(w):
    words, scales = pack_weight(w, "e2m1")
    return words.reshape(words.shape[0], 128, -1), scales


def unpack4(words, scales):
    return unpack_weight(words.reshape(words.shape[0], 128, -1, 2), scales, "e2m1")


E4M3FN = np.array([(-1.0 if i & 128 else 1.0) * ((1.0 + (i & 7) / 8.0) * 2.0 ** (((i >> 3) & 15) - 7) if i & 120 else (i & 7) * 2.0 ** -9) for i in range(256)])


def e4m3fn_bytes(y):
    return np.clip(np.asarray(y, np.float64), -448.0, 448.0).astype(np.float32).astype(ml_dtypes.float8_e4m3fn).view(np.uint8)


def e4m3fn_values(b):
    return E4M3FN[b]


T, D, K = 1024, 512, 1024


def neural_features(x, wq, bias):
    return np.tanh((mxq(x, 1, "e4m3") @ wq) + bias[None, :])


def draw0():
    s, t = mx_kscale(D), mx_kscale(T)
    x0 = bf(np.random.standard_normal((T, D)) * s)
    x1 = bf(np.random.standard_normal((T, D)) * s)
    w_words, w_scales = pack4(np.random.standard_normal((D, K)) / np.sqrt(D) / s[:, None])
    return {
        "x0": x0,
        "x1": x1,
        "w_words": w_words,
        "w_scales": w_scales,
        "bias": bf(0.2 * np.random.standard_normal(K)),
        "a": bf(np.exp(0.3 * np.random.standard_normal(T)) * t),
        "b": bf(np.exp(0.3 * np.random.standard_normal(T)) / t),
    }


def core(x0, x1, w_words, w_scales, bias, a, b):
    x0, x1, bias, a, b = f64(x0), f64(x1), f64(bias), f64(a), f64(b)
    wq = unpack4(w_words, w_scales)
    c0 = neural_features(x0, wq, bias)
    c1 = neural_features(x1, wq, bias)
    p = a * b
    z = np.sum(p)
    m0 = np.sum(p[:, None] * c0, axis=0)
    m1 = np.sum(p[:, None] * c1, axis=0)
    left = a[:, None] * c0
    right = b[:, None] * c1
    s = mxq(left, 0, "e4m3").T @ mxq(right, 0, "e4m3")
    return (s - m0[:, None] * m1[None, :] / z) / np.sqrt(z)


def setup_inputs():
    drawn = draw0()
    full = np.asarray(drawn['x1']).astype(np.float64)
    scale = (np.abs(full).reshape(8, 128, 4, 128).max(axis=(1, 3)) / 448.0).astype(np.float32)
    given = {}
    for key, value in drawn.items():
        if key == 'x1':
            given['x1_bytes'] = e4m3fn_bytes(full / np.repeat(np.repeat(scale.astype(np.float64), 128, axis=0), 128, axis=1))
            given['x1_scale'] = scale
        else:
            given[key] = value
    return given


def reference(x0, x1_bytes, x1_scale, w_words, w_scales, bias, a, b):
    return core(x0, e4m3fn_values(x1_bytes) * np.repeat(np.repeat(x1_scale.astype(np.float64), 128, axis=0), 128, axis=1), w_words, w_scales, bias, a, b)

@@ -1,0 +1,327 @@
+from contextlib import ExitStack
+
+import concourse.mybir as mybir
+from concourse.masks import make_identity
+
+F32 = mybir.dt.float32
+BF16 = mybir.dt.bfloat16
+I32 = mybir.dt.int32
+U32 = mybir.dt.uint32
+U8 = mybir.dt.uint8
+FP8 = mybir.dt.float8_e4m3fn
+FP8X4 = mybir.dt.float8_e4m3fn_x4
+FP4X4 = mybir.dt.float4_e2m1fn_x4
+ALU = mybir.AluOpType
+ACT = mybir.ActivationFunctionType
+AX = mybir.AxisListType
+
+T, D, K = 1024, 512, 1024
+P = 128
+G = 2
+R = 4
+NJ = K // P
+HALF = 512
+
+FLOPS = 2 * (2 * T * D * K) + 2 * T * K * K
+
+UNITS = [("R", 0), ("R", 1), ("R", 2), ("R", 3), ("L", 0), ("R", 4), ("L", 1), ("R", 5), ("L", 2), ("R", 6), ("L", 3), ("R", 7), ("L", 4), ("L", 5), ("L", 6), ("L", 7)]
+TR_BUFS, MM_BUFS, S2_BUFS = 4, 2, 2
+PC_ORDER = 1
+STT_POS = 0
+PER_STEP = 3
+E_LAG = 2
+ON_VEC = {0: (0, 2), 1: (0, 1, 2)}
+ON_ACT = [(c, j) for c in ("R", "L") for j in (1, 3, 5, 7)]
+
+
+def tile_girsanovreweightedneurallagcovariance_d2p_kernel(tc, x0, x1_bytes, x1_scale, w_words, w_scales, bias, a, b, out):
+    nc = tc.nc
+    index = {u: n for n, u in enumerate(UNITS)}
+    steps = len(UNITS)
+
+    with ExitStack() as ctx:
+        keep = ctx.enter_context(tc.tile_pool(name="keep", bufs=1))
+        work = ctx.enter_context(tc.tile_pool(name="work", bufs=3))
+        ps_mm = ctx.enter_context(tc.psum_pool(name="ps_mm", bufs=MM_BUFS))
+        ps_tr = ctx.enter_context(tc.psum_pool(name="ps_tr", bufs=TR_BUFS))
+        ps_s2 = ctx.enter_context(tc.psum_pool(name="ps_s2", bufs=S2_BUFS))
+
+        ident = keep.tile([P, P], F32, name="ident")
+        ones = keep.tile([P, P], F32, name="ones")
+        mhalf = keep.tile([P, 1], F32, name="mhalf")
+        warm = keep.tile([P, 1], F32, name="warm")
+        biasz = keep.tile([P, P], F32, name="biasz")
+        brow = keep.tile([NJ, P], BF16, name="brow")
+        bias_col = keep.tile([P, NJ], F32, name="bias_col")
+        a_col = keep.tile([P, G, R], BF16, name="a_col")
+        b_col = keep.tile([P, G, R], BF16, name="b_col")
+        p_col = keep.tile([P, G * R], F32, name="p_col")
+        p_row = keep.tile([P, G * R, P], F32, name="p_row")
+        zsum = keep.tile([P, 1], F32, name="zsum")
+        zinv = keep.tile([P, 1], F32, name="zinv")
+        rz = keep.tile([P, 1], F32, name="rz")
+        nz = keep.tile([P, 1], F32, name="nz")
+        mcol = {"L": keep.tile([P, NJ], F32, name="mcol_l"), "R": keep.tile([P, NJ], F32, name="mcol_r")}
+        m1row = [keep.tile([P, HALF], F32, name=f"m1row{h}") for h in range(2)]
+        xs = keep.tile([P, G, R], F32, name="xs")
+        wq = keep.tile([P, 2 * K], U8, name="wq", align_bytes=64)
+        ws = keep.tile([P, K], U8, name="ws", align_bytes=64)
+        xbytes = [keep.tile([P, R, D], U8, name=f"xbytes{g}") for g in range(G)]
+        xrow = {c: [keep.tile([P, R, D], BF16, name=f"xrow{c}{g}") for g in range(G)] for c in ("R", "L")}
+        xq = {c: [keep.tile([P, HALF], U32, name=f"xq{c}{g}", align_bytes=64) for g in range(G)] for c in ("R", "L")}
+        xqs = {c: [keep.tile([P, HALF], U8, name=f"xqs{c}{g}", align_bytes=64) for g in range(G)] for c in ("R", "L")}
+        codes = {c: [keep.tile([P, K], U32, name=f"codes{c}{g}", align_bytes=64) for g in range(G)] for c in ("R", "L")}
+        scales = {c: [keep.tile([P, K], U8, name=f"scales{c}{g}", align_bytes=64) for g in range(G)] for c in ("R", "L")}
+        weight_of = {"L": a_col, "R": b_col}
+
+        x1_rows = x1_bytes.rearrange("(g p t) k -> g p t k", p=P, t=R)
+        x0_rows = x0.rearrange("(g p t) k -> g p t k", p=P, t=R)
+        for q in range(4):
+            src = x1_scale.rearrange("(g q) j -> q g j", q=4)[q]
+            nc.scalar.dma_start(out=xs[32 * q : 32 * q + 32, :, :], in_=src.partition_broadcast(32))
+        nc.sync.dma_start(out=xbytes[0][:], in_=x1_rows[0])
+        nc.sync.dma_start(out=xbytes[1][:], in_=x1_rows[1])
+        nc.sync.dma_start(out=wq[:].bitcast(I32), in_=w_words[0].bitcast(I32))
+        make_identity(nc, ident[:])
+        nc.gpsimd.dma_start(out=a_col[:], in_=a.rearrange("(g p t) -> p g t", p=P, t=R))
+        nc.gpsimd.dma_start(out=b_col[:], in_=b.rearrange("(g p t) -> p g t", p=P, t=R))
+        nc.gpsimd.dma_start(out=brow[:], in_=bias.rearrange("(j p) -> j p", p=P))
+        nc.vector.memset(ws[:].bitcast(I32), 0)
+        for q in range(4):
+            nc.sync.dma_start(out=ws[32 * q : 32 * q + 4, :].bitcast(I32), in_=w_scales[0, 4 * q : 4 * q + 4, :].bitcast(I32))
+        for g in range(G):
+            nc.sync.dma_start(out=xrow["L"][g][:], in_=x0_rows[g])
+
+        nc.vector.memset(warm[:], 0.0)
+        nc.scalar.activation(warm[:], warm[:], ACT.Tanh)
+        nc.vector.memset(biasz[:], 0.0)
+        nc.gpsimd.memset(ones[:], 1.0)
+        nc.gpsimd.memset(mhalf[:], -0.5)
+
+        def widen(g):
+            for t in range(R):
+                for j in range(R):
+                    src = xbytes[g][:, t, P * j : P * (j + 1)].bitcast(FP8)
+                    dst = xrow["R"][g][:, t, P * j : P * (j + 1)]
+                    if t in ON_VEC[g]:
+                        nc.vector.tensor_scalar(dst, src, xs[:, g, j : j + 1], None, ALU.mult)
+                    else:
+                        nc.scalar.activation(dst, src, ACT.Copy, scale=xs[:, g, j : j + 1])
+
+        xt_tiles = {}
+
+        def turn(c, g):
+            xt = work.tile([P, HALF, R], BF16, name="xt", align_bytes=64, bufs=2)
+            xt_tiles[(c, g)] = xt
+            for h in range(2):
+                bank = ps_tr.tile([P, 2, 2, P], F32, name="tr")
+                for t in range(2):
+                    for u in range(2):
+                        words = xrow[c][g][:, 2 * h + t, :].bitcast(F32)
+                        nc.tensor.transpose(bank[:, t, u, :], words[:, u : u + D // 2 - 1 : 2], ident[:])
+                dst = xt[:, 256 * h : 256 * (h + 1), :].rearrange("p f e -> p (f e)").bitcast(F32).rearrange("p (t f u) -> p t f u", t=2, u=2)
+                src = bank[:].rearrange("p t u f -> p t f u")
+                if h == 0:
+                    nc.vector.tensor_copy(out=dst, in_=src)
+                else:
+                    nc.scalar.copy(dst, src)
+
+        def quantise_x(c, g):
+            nc.vector.quantize_mx(out=xq[c][g][:].bitcast(FP8X4), scales=xqs[c][g][:], in_=xt_tiles[(c, g)][:].rearrange("p f e -> p (f e)"))
+
+        mm_tiles, ct_tiles, tr_tiles, lq_tiles, pc_tiles, s2_tiles, u_tiles = {}, {}, {}, {}, {}, {}, {}
+
+        def first_product(n, g):
+            c, j = UNITS[n]
+            mm = ps_mm.tile([P, HALF], F32, name="mm")
+            mm_tiles[(n, g)] = mm
+            nc.tensor.matmul_mx(
+                out=mm[:],
+                lhsT=wq[:, 256 * j : 256 * (j + 1)].bitcast(FP4X4),
+                lhsT_scale=ws[:, P * j : P * (j + 1)],
+                rhs=xq[c][g][:].bitcast(FP8X4),
+                rhs_scale=xqs[c][g][:],
+                start=True,
+                stop=True,
+            )
+
+        def tanh(n, g):
+            c, j = UNITS[n]
+            if g == 0:
+                ct_tiles[n] = work.tile([P, G, HALF], F32, name="ct", bufs=3)
+            nc.scalar.activation(ct_tiles[n][:, g, :], mm_tiles[(n, g)][:], ACT.Tanh, bias=bias_col[:, j : j + 1])
+
+        def turn_features(n, g):
+            tr = ps_tr.tile([P, R, P], F32, name="tr")
+            tr_tiles[(n, g)] = tr
+            for t in range(R):
+                nc.tensor.transpose(tr[:, t, :], ct_tiles[n][:, g, P * t : P * (t + 1)], ident[:])
+
+        def weigh(n, g):
+            c, j = UNITS[n]
+            lq = work.tile([P, P, R], BF16, name="lq", align_bytes=64, bufs=4)
+            lq_tiles[(n, g)] = lq
+            wt = weight_of[c][:, g, :].unsqueeze(1).to_broadcast([P, P, R])
+            nc.vector.tensor_tensor(lq[:], tr_tiles[(n, g)][:].rearrange("p t n -> p n t"), wt, ALU.mult)
+
+        def quantise(n, g):
+            c, j = UNITS[n]
+            cols = slice(P * j, P * (j + 1))
+            nc.vector.quantize_mx(out=codes[c][g][:, cols].bitcast(FP8X4), scales=scales[c][g][:, cols], in_=lq_tiles[(n, g)][:].rearrange("p n t -> p (n t)"))
+
+        def moment_on_vector(n):
+            c, j = UNITS[n]
+            junk = work.tile([P, K], BF16, name="junk", bufs=2)
+            nc.vector.scalar_tensor_tensor(
+                out=junk[:],
+                in0=ct_tiles[n][:].rearrange("p g f -> p (g f)"),
+                scalar=1.0,
+                in1=p_row[:].rearrange("p c f -> p (c f)"),
+                op0=ALU.mult,
+                op1=ALU.mult,
+                accum_out=mcol[c][:, j : j + 1],
+            )
+
+        def weigh_p(n, g):
+            pc = work.tile([P, R, P], F32, name="pc", bufs=4)
+            pc_tiles[(n, g)] = pc
+            for t in range(R):
+                q = R * g + t
+                nc.scalar.activation(pc[:, t, :], tr_tiles[(n, g)][:, t, :], ACT.Copy, scale=p_col[:, q : q + 1])
+
+        def sum_p(n):
+            c, j = UNITS[n]
+            acc = ps_s2.tile([P, HALF], F32, name="s2")
+            for g in range(G):
+                for t in range(R):
+                    nc.tensor.matmul(acc[:, 0:P], pc_tiles[(n, g)][:, t, :], ident[:], start=(g == 0 and t == 0), stop=(g == G - 1 and t == R - 1), is_transpose=True)
+            nc.vector.tensor_reduce(mcol[c][:, j : j + 1], acc[:, 0:P], AX.X, ALU.add)
+
+        def spread_m1(h):
+            bank = ps_s2.tile([P, HALF], F32, name="s2")
+            for j in range(4):
+                col = mcol["R"][:, 4 * h + j : 4 * h + j + 1]
+                nc.tensor.transpose(bank[:, P * j : P * (j + 1)], col.to_broadcast([P, P]), ident[:])
+            nc.scalar.activation(m1row[h][:], bank[:], ACT.Copy, scale=nz[:])
+
+        def second_product(i, h):
+            s2 = ps_s2.tile([P, HALF], F32, name="s2")
+            s2_tiles[(i, h)] = s2
+            for g in range(G):
+                nc.tensor.matmul_mx(
+                    out=s2[:],
+                    lhsT=codes["L"][g][:, P * i : P * (i + 1)].bitcast(FP8X4),
+                    lhsT_scale=scales["L"][g][:, P * i : P * (i + 1)],
+                    rhs=codes["R"][g][:, HALF * h : HALF * (h + 1)].bitcast(FP8X4),
+                    rhs_scale=scales["R"][g][:, HALF * h : HALF * (h + 1)],
+                    start=(g == 0),
+                    stop=(g == G - 1),
+                )
+
+        def outer(i, h):
+            ut = work.tile([P, HALF], F32, name="ut", bufs=4)
+            u_tiles[(i, h)] = ut
+            nc.gpsimd.tensor_scalar(ut[:], m1row[h][:], mcol["L"][:, i : i + 1], 0.0, ALU.mult, ALU.add)
+
+        def finish(i, h):
+            ot = work.tile([P, HALF], F32, name="ot", bufs=4)
+            nc.vector.scalar_tensor_tensor(out=ot[:], in0=s2_tiles[(i, h)][:], scalar=rz[:], in1=u_tiles[(i, h)][:], op0=ALU.mult, op1=ALU.add)
+            nc.sync.dma_start(out=out[P * i : P * (i + 1), HALF * h : HALF * (h + 1)], in_=ot[:])
+
+        ready = {}
+        for h in range(2):
+            last = max(index[("R", j)] + (2 if ("R", j) in ON_ACT else 1) for j in range(4 * h, 4 * h + 4))
+            ready[h] = last
+        plan = {}
+        order = sorted(((max(index[("L", i)] + E_LAG, ready[h] + 1, index[("R", 4 * h + 3)] + 2), h, i) for h in range(2) for i in range(NJ)))
+        step_at = 0
+        count = 0
+        for first, h, i in order:
+            s = max(first, step_at)
+            if s > step_at:
+                step_at, count = s, 0
+            plan.setdefault(step_at, []).append((i, h))
+            count += 1
+            if count == PER_STEP:
+                step_at, count = step_at + 1, 0
+
+        def spread_p():
+            for h in range(2):
+                bank = ps_tr.tile([P, R, P], F32, name="tr")
+                for t in range(R):
+                    q = R * h + t
+                    nc.tensor.transpose(bank[:, t, :], p_col[:, q : q + 1].to_broadcast([P, P]), ident[:])
+                nc.scalar.copy(p_row[:, R * h : R * (h + 1), :], bank[:])
+
+        widen(0)
+        widen(1)
+        nc.vector.tensor_tensor(p_col[:], a_col[:].rearrange("p g t -> p (g t)"), b_col[:].rearrange("p g t -> p (g t)"), ALU.mult)
+        nc.vector.tensor_copy(out=biasz[0:NJ, :], in_=brow[:])
+        turn("R", 0)
+        mi = ps_s2.tile([P, HALF], F32, name="s2")
+        nc.tensor.transpose(mi[:, 0:P], biasz[:], ident[:])
+        nc.scalar.copy(bias_col[:], mi[:, 0:NJ])
+        turn("R", 1)
+        quantise_x("R", 0)
+        turn("L", 0)
+        quantise_x("R", 1)
+        first_product(0, 0)
+        first_product(0, 1)
+        tanh(0, 0)
+        tanh(0, 1)
+        mz = ps_s2.tile([P, HALF], F32, name="s2")
+        nc.tensor.matmul(mz[:, 0 : G * R], ones[:], p_col[:], start=True, stop=True)
+        spread_p()
+        quantise_x("L", 0)
+        nc.vector.tensor_reduce(zsum[:], mz[:, 0 : G * R], AX.X, ALU.add)
+        turn("L", 1)
+        nc.vector.reciprocal(zinv[:], zsum[:])
+        nc.gpsimd.tensor_tensor(rz[:], zsum[:], mhalf[:], ALU.pow)
+        nc.gpsimd.tensor_tensor(nz[:], rz[:], zinv[:], ALU.mult)
+        nc.gpsimd.tensor_scalar(nz[:], nz[:], -1.0, 0.0, ALU.mult, ALU.add)
+        quantise_x("L", 1)
+
+        for s in range(steps + 3):
+            tasks = plan.get(s, [])
+            if s + 1 < steps:
+                for g in range(G):
+                    first_product(s + 1, g)
+            for h in range(2):
+                if ready[h] == s:
+                    spread_m1(h)
+            for i, h in tasks:
+                second_product(i, h)
+                outer(i, h)
+            prev = 1 <= s <= steps
+            prev_on_act = prev and UNITS[s - 1] in ON_ACT
+            on_act = [("pc", 1), ("th", 0), ("pc", 0), ("th", 1)] if PC_ORDER == 0 else [("pc", 1), ("pc", 0), ("th", 0), ("th", 1)] if PC_ORDER == 1 else [("th", 0), ("pc", 1), ("pc", 0), ("th", 1)]
+            for what, g in on_act:
+                if what == "pc" and prev_on_act:
+                    weigh_p(s - 1, g)
+                if what == "th" and s + 1 < steps:
+                    tanh(s + 1, g)
+            stt = s < steps and UNITS[s] not in ON_ACT
+            if stt and STT_POS == 0:
+                moment_on_vector(s)
+            if prev:
+                weigh(s - 1, 0)
+            if len(tasks) > 0:
+                finish(*tasks[0])
+            if prev:
+                weigh(s - 1, 1)
+                quantise(s - 1, 0)
+            if stt and STT_POS == 1:
+                moment_on_vector(s)
+            if len(tasks) > 1:
+                finish(*tasks[1])
+            if prev:
+                quantise(s - 1, 1)
+            if stt and STT_POS == 2:
+                moment_on_vector(s)
+            for task in tasks[2:]:
+                finish(*task)
+            if s < steps:
+                for g in range(G):
+                    turn_features(s, g)
+            if prev_on_act:
+                sum_p(s - 1)

@@ -13,134 +13,162 @@ FP8X4 = mybir.dt.float8_e4m3fn_x4
 FP4X4 = mybir.dt.float4_e2m1fn_x4
 ALU = mybir.AluOpType
 ACT = mybir.ActivationFunctionType
-AX = mybir.AxisListType
+X_AXIS = mybir.AxisListType.X
 
 T, D, K = 1024, 512, 1024
 P = 128
-G = 2
 R = 4
-NJ = K // P
 HALF = 512
+G = T // HALF
+NJ = K // P
+HALF_TILES = HALF // P
 
 FLOPS = 2 * (2 * T * D * K) + 2 * T * K * K
 
-UNITS = [("R", 0), ("R", 1), ("R", 2), ("R", 3), ("L", 0), ("R", 4), ("L", 1), ("R", 5), ("L", 2), ("R", 6), ("L", 3), ("R", 7), ("L", 4), ("L", 5), ("L", 6), ("L", 7)]
-TR_BUFS, MM_BUFS, S2_BUFS = 4, 2, 2
-PC_ORDER = 1
-STT_POS = 0
-PER_STEP = 3
-E_LAG = 2
-ON_VEC = {0: (0, 2), 1: (0, 1, 2)}
-ON_ACT = [(c, j) for c in ("R", "L") for j in (1, 3, 5, 7)]
+UNITS = [("R", 0), ("R", 1), ("R", 2), ("R", 3), ("L", 0), ("R", 4), ("L", 1), ("R", 5), ("L", 2), ("R", 6), ("R", 7), ("L", 3), ("L", 4), ("L", 5), ("L", 6), ("L", 7)]
+ON_SCALAR = [("R", 2), ("R", 4), ("R", 5), ("R", 6), ("L", 5), ("L", 6)]
+Z_STEP = 2
+BLOCKS_PER_STEP = 2
 
 
 def tile_girsanovreweightedneurallagcovariance_d2p_kernel(tc, x0, x1_bytes, x1_scale, w_words, w_scales, bias, a, b, out):
     nc = tc.nc
-    index = {u: n for n, u in enumerate(UNITS)}
-    steps = len(UNITS)
+    units = len(UNITS)
+    position = {unit: n for n, unit in enumerate(UNITS)}
 
     with ExitStack() as ctx:
         keep = ctx.enter_context(tc.tile_pool(name="keep", bufs=1))
-        work = ctx.enter_context(tc.tile_pool(name="work", bufs=3))
-        ps_mm = ctx.enter_context(tc.psum_pool(name="ps_mm", bufs=MM_BUFS))
-        ps_tr = ctx.enter_context(tc.psum_pool(name="ps_tr", bufs=TR_BUFS))
-        ps_s2 = ctx.enter_context(tc.psum_pool(name="ps_s2", bufs=S2_BUFS))
+        work = ctx.enter_context(tc.tile_pool(name="work", bufs=4))
+        psum_first = ctx.enter_context(tc.psum_pool(name="psum_first", bufs=2))
+        psum_turn = ctx.enter_context(tc.psum_pool(name="psum_turn", bufs=4))
+        psum_out = ctx.enter_context(tc.psum_pool(name="psum_out", bufs=2))
+        ctx.enter_context(tc.manual_schedule())
 
         ident = keep.tile([P, P], F32, name="ident")
         ones = keep.tile([P, P], F32, name="ones")
-        mhalf = keep.tile([P, 1], F32, name="mhalf")
-        warm = keep.tile([P, 1], F32, name="warm")
-        biasz = keep.tile([P, P], F32, name="biasz")
-        brow = keep.tile([NJ, P], BF16, name="brow")
+        minus_half = keep.tile([P, 1], F32, name="minus_half")
+        first_tanh = keep.tile([P, 1], F32, name="first_tanh")
+        bias_square = keep.tile([P, P], F32, name="bias_square")
+        bias_rows = keep.tile([NJ, P], BF16, name="bias_rows")
         bias_col = keep.tile([P, NJ], F32, name="bias_col")
         a_col = keep.tile([P, G, R], BF16, name="a_col")
         b_col = keep.tile([P, G, R], BF16, name="b_col")
         p_col = keep.tile([P, G * R], F32, name="p_col")
         p_row = keep.tile([P, G * R, P], F32, name="p_row")
-        zsum = keep.tile([P, 1], F32, name="zsum")
-        zinv = keep.tile([P, 1], F32, name="zinv")
-        rz = keep.tile([P, 1], F32, name="rz")
-        nz = keep.tile([P, 1], F32, name="nz")
-        mcol = {"L": keep.tile([P, NJ], F32, name="mcol_l"), "R": keep.tile([P, NJ], F32, name="mcol_r")}
-        m1row = [keep.tile([P, HALF], F32, name=f"m1row{h}") for h in range(2)]
-        xs = keep.tile([P, G, R], F32, name="xs")
-        wq = keep.tile([P, 2 * K], U8, name="wq", align_bytes=64)
-        ws = keep.tile([P, K], U8, name="ws", align_bytes=64)
-        xbytes = [keep.tile([P, R, D], U8, name=f"xbytes{g}") for g in range(G)]
-        xrow = {c: [keep.tile([P, R, D], BF16, name=f"xrow{c}{g}") for g in range(G)] for c in ("R", "L")}
-        xq = {c: [keep.tile([P, HALF], U32, name=f"xq{c}{g}", align_bytes=64) for g in range(G)] for c in ("R", "L")}
-        xqs = {c: [keep.tile([P, HALF], U8, name=f"xqs{c}{g}", align_bytes=64) for g in range(G)] for c in ("R", "L")}
+        z = keep.tile([P, 1], F32, name="z")
+        z_inv = keep.tile([P, 1], F32, name="z_inv")
+        z_rsqrt = keep.tile([P, 1], F32, name="z_rsqrt")
+        term_scale = keep.tile([P, 1], F32, name="term_scale")
+        moment = {c: keep.tile([P, NJ], F32, name=f"moment{c}") for c in ("L", "R")}
+        m1_row = [keep.tile([P, HALF], F32, name=f"m1_row{h}") for h in range(2)]
+        x1_scales = keep.tile([P, G, R], F32, name="x1_scales")
+        w_codes = keep.tile([P, 2 * K], U8, name="w_codes", align_bytes=64)
+        w_planes = keep.tile([P, K], U8, name="w_planes", align_bytes=64)
+        x1_in = [keep.tile([P, R, D], U8, name=f"x1_in{g}") for g in range(G)]
+        x0_in = [keep.tile([P, R, D], BF16, name=f"x0_in{g}") for g in range(G)]
+        pairs = {c: [keep.tile([P, R, 2, P, 2], BF16, name=f"pairs{c}{g}") for g in range(G)] for c in ("R", "L")}
+        x_codes = {c: [keep.tile([P, HALF], U32, name=f"x_codes{c}{g}", align_bytes=64) for g in range(G)] for c in ("R", "L")}
+        x_planes = {c: [keep.tile([P, HALF], U8, name=f"x_planes{c}{g}", align_bytes=64) for g in range(G)] for c in ("R", "L")}
         codes = {c: [keep.tile([P, K], U32, name=f"codes{c}{g}", align_bytes=64) for g in range(G)] for c in ("R", "L")}
-        scales = {c: [keep.tile([P, K], U8, name=f"scales{c}{g}", align_bytes=64) for g in range(G)] for c in ("R", "L")}
-        weight_of = {"L": a_col, "R": b_col}
+        planes = {c: [keep.tile([P, K], U8, name=f"planes{c}{g}", align_bytes=64) for g in range(G)] for c in ("R", "L")}
+        frame_weight = {"L": a_col, "R": b_col}
 
         x1_rows = x1_bytes.rearrange("(g p t) k -> g p t k", p=P, t=R)
         x0_rows = x0.rearrange("(g p t) k -> g p t k", p=P, t=R)
+        scale_rows = x1_scale.rearrange("(g q) j -> q g j", q=4)
         for q in range(4):
-            src = x1_scale.rearrange("(g q) j -> q g j", q=4)[q]
-            nc.scalar.dma_start(out=xs[32 * q : 32 * q + 32, :, :], in_=src.partition_broadcast(32))
-        nc.sync.dma_start(out=xbytes[0][:], in_=x1_rows[0])
-        nc.sync.dma_start(out=xbytes[1][:], in_=x1_rows[1])
-        nc.sync.dma_start(out=wq[:].bitcast(I32), in_=w_words[0].bitcast(I32))
+            nc.scalar.dma_start(out=x1_scales[32 * q : 32 * q + 32, :, :], in_=scale_rows[q].partition_broadcast(32))
+        nc.sync.dma_start(out=x1_in[0][:], in_=x1_rows[0])
+        nc.sync.dma_start(out=x1_in[1][:], in_=x1_rows[1])
+        nc.sync.dma_start(out=w_codes[:].bitcast(I32), in_=w_words[0].bitcast(I32))
+        nc.gpsimd.memset(ones[:], 1.0)
         make_identity(nc, ident[:])
         nc.gpsimd.dma_start(out=a_col[:], in_=a.rearrange("(g p t) -> p g t", p=P, t=R))
         nc.gpsimd.dma_start(out=b_col[:], in_=b.rearrange("(g p t) -> p g t", p=P, t=R))
-        nc.gpsimd.dma_start(out=brow[:], in_=bias.rearrange("(j p) -> j p", p=P))
-        nc.vector.memset(ws[:].bitcast(I32), 0)
+        nc.gpsimd.dma_start(out=bias_rows[:], in_=bias.rearrange("(j p) -> j p", p=P))
+        nc.vector.memset(w_planes[:].bitcast(I32), 0)
         for q in range(4):
-            nc.sync.dma_start(out=ws[32 * q : 32 * q + 4, :].bitcast(I32), in_=w_scales[0, 4 * q : 4 * q + 4, :].bitcast(I32))
+            nc.sync.dma_start(out=w_planes[32 * q : 32 * q + 4, :].bitcast(I32), in_=w_scales[0, 4 * q : 4 * q + 4, :].bitcast(I32))
         for g in range(G):
-            nc.sync.dma_start(out=xrow["L"][g][:], in_=x0_rows[g])
+            nc.sync.dma_start(out=x0_in[g][:], in_=x0_rows[g])
+        nc.vector.memset(first_tanh[:], 0.0)
+        nc.scalar.activation(first_tanh[:], first_tanh[:], ACT.Tanh)
+        nc.vector.memset(bias_square[:], 0.0)
+        nc.gpsimd.memset(minus_half[:], -0.5)
 
-        nc.vector.memset(warm[:], 0.0)
-        nc.scalar.activation(warm[:], warm[:], ACT.Tanh)
-        nc.vector.memset(biasz[:], 0.0)
-        nc.gpsimd.memset(ones[:], 1.0)
-        nc.gpsimd.memset(mhalf[:], -0.5)
-
-        def widen(g):
+        def widen_x1(g):
             for t in range(R):
-                for j in range(R):
-                    src = xbytes[g][:, t, P * j : P * (j + 1)].bitcast(FP8)
-                    dst = xrow["R"][g][:, t, P * j : P * (j + 1)]
-                    if t in ON_VEC[g]:
-                        nc.vector.tensor_scalar(dst, src, xs[:, g, j : j + 1], None, ALU.mult)
-                    else:
-                        nc.scalar.activation(dst, src, ACT.Copy, scale=xs[:, g, j : j + 1])
+                for j in range(D // P):
+                    src = x1_in[g][:, t, P * j : P * (j + 1)].bitcast(FP8).rearrange("p (q u e) -> p q u e", u=2, e=2)
+                    dst = pairs["R"][g][:, t, :, 32 * j : 32 * (j + 1), :].rearrange("p u q e -> p q u e")
+                    nc.vector.tensor_scalar(dst, src, x1_scales[:, g, j : j + 1], None, ALU.mult)
 
-        xt_tiles = {}
+        def sort_x0(g):
+            dst = pairs["L"][g][:].rearrange("p t u q e -> p (t u q e)").bitcast(F32).rearrange("p (t u q) -> p t u q", t=R, u=2)
+            src = x0_in[g][:].rearrange("p t k -> p (t k)").bitcast(F32).rearrange("p (t q u) -> p t u q", t=R, u=2)
+            nc.vector.tensor_copy(out=dst, in_=src)
 
-        def turn(c, g):
-            xt = work.tile([P, HALF, R], BF16, name="xt", align_bytes=64, bufs=2)
-            xt_tiles[(c, g)] = xt
-            for h in range(2):
-                bank = ps_tr.tile([P, 2, 2, P], F32, name="tr")
-                for t in range(2):
-                    for u in range(2):
-                        words = xrow[c][g][:, 2 * h + t, :].bitcast(F32)
-                        nc.tensor.transpose(bank[:, t, u, :], words[:, u : u + D // 2 - 1 : 2], ident[:])
-                dst = xt[:, 256 * h : 256 * (h + 1), :].rearrange("p f e -> p (f e)").bitcast(F32).rearrange("p (t f u) -> p t f u", t=2, u=2)
-                src = bank[:].rearrange("p t u f -> p t f u")
-                if h == 0:
-                    nc.vector.tensor_copy(out=dst, in_=src)
-                else:
-                    nc.scalar.copy(dst, src)
+        turned = {}
+        x_rows = {}
+
+        def turn_x(c, g, h):
+            bank = psum_turn.tile([P, 2, 2, P], F32, name="turn")
+            turned[(c, g, h)] = bank
+            for t in range(2):
+                for u in range(2):
+                    words = pairs[c][g][:, 2 * h + t, u, :, :].rearrange("p q e -> p (q e)").bitcast(F32)
+                    nc.tensor.transpose(bank[:, t, u, :], words, ident[:])
+
+        def interleave_x(c, g, h):
+            if h == 0:
+                x_rows[(c, g)] = work.tile([P, HALF, R], BF16, name="x_rows", align_bytes=64)
+            frames = x_rows[(c, g)][:, 2 * P * h : 2 * P * (h + 1), :]
+            dst = frames.rearrange("p f e -> p (f e)").bitcast(F32).rearrange("p (t f u) -> p t f u", t=2, u=2)
+            nc.scalar.copy(dst, turned[(c, g, h)][:].rearrange("p t u f -> p t f u"))
 
         def quantise_x(c, g):
-            nc.vector.quantize_mx(out=xq[c][g][:].bitcast(FP8X4), scales=xqs[c][g][:], in_=xt_tiles[(c, g)][:].rearrange("p f e -> p (f e)"))
+            nc.vector.quantize_mx(out=x_codes[c][g][:].bitcast(FP8X4), scales=x_planes[c][g][:], in_=x_rows[(c, g)][:].rearrange("p f e -> p (f e)"))
 
-        mm_tiles, ct_tiles, tr_tiles, lq_tiles, pc_tiles, s2_tiles, u_tiles = {}, {}, {}, {}, {}, {}, {}
+        def spread(bank, column, col):
+            nc.tensor.transpose(bank[:, column : column + P], col.to_broadcast([P, P]), ident[:])
+
+        def path_weights():
+            nc.vector.tensor_tensor(p_col[:], a_col[:].rearrange("p g t -> p (g t)"), b_col[:].rearrange("p g t -> p (g t)"), ALU.mult)
+            banks = []
+            for g in range(G):
+                bank = psum_turn.tile([P, HALF], F32, name="turn")
+                banks.append(bank)
+                for t in range(R):
+                    spread(bank, P * t, p_col[:, R * g + t : R * g + t + 1])
+            for g in range(G):
+                nc.scalar.copy(p_row[:, R * g : R * (g + 1), :].rearrange("p c f -> p (c f)"), banks[g][:])
+
+        def place_bias():
+            nc.vector.tensor_copy(out=bias_square[0:NJ, :], in_=bias_rows[:])
+            bank = psum_out.tile([P, HALF], F32, name="out_bank")
+            nc.tensor.transpose(bank[:, 0:P], bias_square[:], ident[:])
+            nc.scalar.copy(bias_col[:], bank[:, 0:NJ])
+
+        def sum_of_weights():
+            bank = psum_out.tile([P, HALF], F32, name="out_bank")
+            nc.tensor.matmul(bank[:, 0 : G * R], ones[:], p_col[:], start=True, stop=True)
+            nc.vector.tensor_reduce(z[:], bank[:, 0 : G * R], X_AXIS, ALU.add)
+            nc.vector.reciprocal(z_inv[:], z[:])
+            nc.gpsimd.tensor_tensor(z_rsqrt[:], z[:], minus_half[:], ALU.pow)
+            nc.gpsimd.tensor_tensor(term_scale[:], z_rsqrt[:], z_inv[:], ALU.mult)
+            nc.gpsimd.tensor_scalar(term_scale[:], term_scale[:], -1.0, 0.0, ALU.mult, ALU.add)
+
+        first, features, turned_features, weighted, p_weighted = {}, {}, {}, {}, {}
 
         def first_product(n, g):
             c, j = UNITS[n]
-            mm = ps_mm.tile([P, HALF], F32, name="mm")
-            mm_tiles[(n, g)] = mm
+            first[(n, g)] = psum_first.tile([P, HALF], F32, name="first_bank")
             nc.tensor.matmul_mx(
-                out=mm[:],
-                lhsT=wq[:, 256 * j : 256 * (j + 1)].bitcast(FP4X4),
-                lhsT_scale=ws[:, P * j : P * (j + 1)],
-                rhs=xq[c][g][:].bitcast(FP8X4),
-                rhs_scale=xqs[c][g][:],
+                out=first[(n, g)][:],
+                lhsT=w_codes[:, 2 * P * j : 2 * P * (j + 1)].bitcast(FP4X4),
+                lhsT_scale=w_planes[:, P * j : P * (j + 1)],
+                rhs=x_codes[c][g][:].bitcast(FP8X4),
+                rhs_scale=x_planes[c][g][:],
                 start=True,
                 stop=True,
             )
@@ -148,180 +176,149 @@ def tile_girsanovreweightedneurallagcovariance_d2p_kernel(tc, x0, x1_bytes, x1_s
         def tanh(n, g):
             c, j = UNITS[n]
             if g == 0:
-                ct_tiles[n] = work.tile([P, G, HALF], F32, name="ct", bufs=3)
-            nc.scalar.activation(ct_tiles[n][:, g, :], mm_tiles[(n, g)][:], ACT.Tanh, bias=bias_col[:, j : j + 1])
+                features[n] = work.tile([P, G, HALF], F32, name="features")
+            nc.scalar.activation(features[n][:, g, :], first[(n, g)][:], ACT.Tanh, bias=bias_col[:, j : j + 1])
 
         def turn_features(n, g):
-            tr = ps_tr.tile([P, R, P], F32, name="tr")
-            tr_tiles[(n, g)] = tr
+            turned_features[(n, g)] = psum_turn.tile([P, R, P], F32, name="turn")
             for t in range(R):
-                nc.tensor.transpose(tr[:, t, :], ct_tiles[n][:, g, P * t : P * (t + 1)], ident[:])
+                nc.tensor.transpose(turned_features[(n, g)][:, t, :], features[n][:, g, P * t : P * (t + 1)], ident[:])
 
         def weigh(n, g):
             c, j = UNITS[n]
-            lq = work.tile([P, P, R], BF16, name="lq", align_bytes=64, bufs=4)
-            lq_tiles[(n, g)] = lq
-            wt = weight_of[c][:, g, :].unsqueeze(1).to_broadcast([P, P, R])
-            nc.vector.tensor_tensor(lq[:], tr_tiles[(n, g)][:].rearrange("p t n -> p n t"), wt, ALU.mult)
+            weighted[(n, g)] = work.tile([P, P, R], BF16, name="weighted", align_bytes=64)
+            weights = frame_weight[c][:, g, :].unsqueeze(1).to_broadcast([P, P, R])
+            nc.vector.tensor_tensor(weighted[(n, g)][:], turned_features[(n, g)][:].rearrange("p t n -> p n t"), weights, ALU.mult)
 
         def quantise(n, g):
             c, j = UNITS[n]
             cols = slice(P * j, P * (j + 1))
-            nc.vector.quantize_mx(out=codes[c][g][:, cols].bitcast(FP8X4), scales=scales[c][g][:, cols], in_=lq_tiles[(n, g)][:].rearrange("p n t -> p (n t)"))
+            nc.vector.quantize_mx(out=codes[c][g][:, cols].bitcast(FP8X4), scales=planes[c][g][:, cols], in_=weighted[(n, g)][:].rearrange("p n t -> p (n t)"))
 
         def moment_on_vector(n):
             c, j = UNITS[n]
-            junk = work.tile([P, K], BF16, name="junk", bufs=2)
+            product = work.tile([P, T], BF16, name="product")
             nc.vector.scalar_tensor_tensor(
-                out=junk[:],
-                in0=ct_tiles[n][:].rearrange("p g f -> p (g f)"),
+                out=product[:],
+                in0=features[n][:].rearrange("p g f -> p (g f)"),
                 scalar=1.0,
                 in1=p_row[:].rearrange("p c f -> p (c f)"),
                 op0=ALU.mult,
                 op1=ALU.mult,
-                accum_out=mcol[c][:, j : j + 1],
+                accum_out=moment[c][:, j : j + 1],
             )
 
-        def weigh_p(n, g):
-            pc = work.tile([P, R, P], F32, name="pc", bufs=4)
-            pc_tiles[(n, g)] = pc
+        def times_p(n, g):
+            p_weighted[(n, g)] = work.tile([P, R, P], F32, name="p_weighted")
             for t in range(R):
-                q = R * g + t
-                nc.scalar.activation(pc[:, t, :], tr_tiles[(n, g)][:, t, :], ACT.Copy, scale=p_col[:, q : q + 1])
+                nc.scalar.activation(p_weighted[(n, g)][:, t, :], turned_features[(n, g)][:, t, :], ACT.Copy, scale=p_col[:, R * g + t : R * g + t + 1])
 
-        def sum_p(n):
+        def moment_on_scalar(n):
             c, j = UNITS[n]
-            acc = ps_s2.tile([P, HALF], F32, name="s2")
+            bank = psum_out.tile([P, HALF], F32, name="out_bank")
             for g in range(G):
                 for t in range(R):
-                    nc.tensor.matmul(acc[:, 0:P], pc_tiles[(n, g)][:, t, :], ident[:], start=(g == 0 and t == 0), stop=(g == G - 1 and t == R - 1), is_transpose=True)
-            nc.vector.tensor_reduce(mcol[c][:, j : j + 1], acc[:, 0:P], AX.X, ALU.add)
+                    slot = R * g + t
+                    nc.tensor.matmul(bank[:, 0:P], p_weighted[(n, g)][:, t, :], ident[:], start=(slot == 0), stop=(slot == G * R - 1), is_transpose=True)
+            sums = work.tile([P, P], BF16, name="sums")
+            nc.scalar.activation(sums[:], bank[:, 0:P], ACT.Copy, accum_out=moment[c][:, j : j + 1])
 
-        def spread_m1(h):
-            bank = ps_s2.tile([P, HALF], F32, name="s2")
-            for j in range(4):
-                col = mcol["R"][:, 4 * h + j : 4 * h + j + 1]
-                nc.tensor.transpose(bank[:, P * j : P * (j + 1)], col.to_broadcast([P, P]), ident[:])
-            nc.scalar.activation(m1row[h][:], bank[:], ACT.Copy, scale=nz[:])
+        def m1_to_row(h):
+            bank = psum_out.tile([P, HALF], F32, name="out_bank")
+            for j in range(HALF_TILES):
+                spread(bank, P * j, moment["R"][:, HALF_TILES * h + j : HALF_TILES * h + j + 1])
+            nc.scalar.activation(m1_row[h][:], bank[:], ACT.Copy, scale=term_scale[:])
 
-        def second_product(i, h):
-            s2 = ps_s2.tile([P, HALF], F32, name="s2")
-            s2_tiles[(i, h)] = s2
+        rank_one = {}
+
+        def rank_one_term(i, h):
+            rank_one[(i, h)] = work.tile([P, HALF], F32, name="rank_one")
+            nc.scalar.activation(rank_one[(i, h)][:], m1_row[h][:], ACT.Copy, scale=moment["L"][:, i : i + 1])
+
+        def finish_block(i, h):
+            bank = psum_out.tile([P, HALF], F32, name="out_bank")
+            rows = slice(P * i, P * (i + 1))
+            cols = slice(HALF * h, HALF * (h + 1))
             for g in range(G):
                 nc.tensor.matmul_mx(
-                    out=s2[:],
-                    lhsT=codes["L"][g][:, P * i : P * (i + 1)].bitcast(FP8X4),
-                    lhsT_scale=scales["L"][g][:, P * i : P * (i + 1)],
-                    rhs=codes["R"][g][:, HALF * h : HALF * (h + 1)].bitcast(FP8X4),
-                    rhs_scale=scales["R"][g][:, HALF * h : HALF * (h + 1)],
+                    out=bank[:],
+                    lhsT=codes["L"][g][:, rows].bitcast(FP8X4),
+                    lhsT_scale=planes["L"][g][:, rows],
+                    rhs=codes["R"][g][:, cols].bitcast(FP8X4),
+                    rhs_scale=planes["R"][g][:, cols],
                     start=(g == 0),
                     stop=(g == G - 1),
                 )
+            result = work.tile([P, HALF], F32, name="result", bufs=6)
+            nc.vector.scalar_tensor_tensor(out=result[:], in0=bank[:], scalar=z_rsqrt[:], in1=rank_one[(i, h)][:], op0=ALU.mult, op1=ALU.add)
+            nc.sync.dma_start(out=out[rows, cols], in_=result[:])
 
-        def outer(i, h):
-            ut = work.tile([P, HALF], F32, name="ut", bufs=4)
-            u_tiles[(i, h)] = ut
-            nc.gpsimd.tensor_scalar(ut[:], m1row[h][:], mcol["L"][:, i : i + 1], 0.0, ALU.mult, ALU.add)
-
-        def finish(i, h):
-            ot = work.tile([P, HALF], F32, name="ot", bufs=4)
-            nc.vector.scalar_tensor_tensor(out=ot[:], in0=s2_tiles[(i, h)][:], scalar=rz[:], in1=u_tiles[(i, h)][:], op0=ALU.mult, op1=ALU.add)
-            nc.sync.dma_start(out=out[P * i : P * (i + 1), HALF * h : HALF * (h + 1)], in_=ot[:])
-
-        ready = {}
-        for h in range(2):
-            last = max(index[("R", j)] + (2 if ("R", j) in ON_ACT else 1) for j in range(4 * h, 4 * h + 4))
-            ready[h] = last
-        plan = {}
-        order = sorted(((max(index[("L", i)] + E_LAG, ready[h] + 1, index[("R", 4 * h + 3)] + 2), h, i) for h in range(2) for i in range(NJ)))
-        step_at = 0
-        count = 0
-        for first, h, i in order:
-            s = max(first, step_at)
-            if s > step_at:
-                step_at, count = s, 0
-            plan.setdefault(step_at, []).append((i, h))
-            count += 1
-            if count == PER_STEP:
-                step_at, count = step_at + 1, 0
-
-        def spread_p():
+        for g in range(G):
+            widen_x1(g)
+        for g in range(G):
             for h in range(2):
-                bank = ps_tr.tile([P, R, P], F32, name="tr")
-                for t in range(R):
-                    q = R * h + t
-                    nc.tensor.transpose(bank[:, t, :], p_col[:, q : q + 1].to_broadcast([P, P]), ident[:])
-                nc.scalar.copy(p_row[:, R * h : R * (h + 1), :], bank[:])
-
-        widen(0)
-        widen(1)
-        nc.vector.tensor_tensor(p_col[:], a_col[:].rearrange("p g t -> p (g t)"), b_col[:].rearrange("p g t -> p (g t)"), ALU.mult)
-        nc.vector.tensor_copy(out=biasz[0:NJ, :], in_=brow[:])
-        turn("R", 0)
-        mi = ps_s2.tile([P, HALF], F32, name="s2")
-        nc.tensor.transpose(mi[:, 0:P], biasz[:], ident[:])
-        nc.scalar.copy(bias_col[:], mi[:, 0:NJ])
-        turn("R", 1)
-        quantise_x("R", 0)
-        turn("L", 0)
-        quantise_x("R", 1)
-        first_product(0, 0)
-        first_product(0, 1)
-        tanh(0, 0)
-        tanh(0, 1)
-        mz = ps_s2.tile([P, HALF], F32, name="s2")
-        nc.tensor.matmul(mz[:, 0 : G * R], ones[:], p_col[:], start=True, stop=True)
-        spread_p()
-        quantise_x("L", 0)
-        nc.vector.tensor_reduce(zsum[:], mz[:, 0 : G * R], AX.X, ALU.add)
-        turn("L", 1)
-        nc.vector.reciprocal(zinv[:], zsum[:])
-        nc.gpsimd.tensor_tensor(rz[:], zsum[:], mhalf[:], ALU.pow)
-        nc.gpsimd.tensor_tensor(nz[:], rz[:], zinv[:], ALU.mult)
-        nc.gpsimd.tensor_scalar(nz[:], nz[:], -1.0, 0.0, ALU.mult, ALU.add)
-        quantise_x("L", 1)
-
-        for s in range(steps + 3):
-            tasks = plan.get(s, [])
-            if s + 1 < steps:
-                for g in range(G):
-                    first_product(s + 1, g)
+                turn_x("R", g, h)
+                interleave_x("R", g, h)
+        path_weights()
+        for g in range(G):
+            sort_x0(g)
+        place_bias()
+        for g in range(G):
+            quantise_x("R", g)
             for h in range(2):
-                if ready[h] == s:
-                    spread_m1(h)
-            for i, h in tasks:
-                second_product(i, h)
-                outer(i, h)
-            prev = 1 <= s <= steps
-            prev_on_act = prev and UNITS[s - 1] in ON_ACT
-            on_act = [("pc", 1), ("th", 0), ("pc", 0), ("th", 1)] if PC_ORDER == 0 else [("pc", 1), ("pc", 0), ("th", 0), ("th", 1)] if PC_ORDER == 1 else [("th", 0), ("pc", 1), ("pc", 0), ("th", 1)]
-            for what, g in on_act:
-                if what == "pc" and prev_on_act:
-                    weigh_p(s - 1, g)
-                if what == "th" and s + 1 < steps:
-                    tanh(s + 1, g)
-            stt = s < steps and UNITS[s] not in ON_ACT
-            if stt and STT_POS == 0:
-                moment_on_vector(s)
-            if prev:
-                weigh(s - 1, 0)
-            if len(tasks) > 0:
-                finish(*tasks[0])
-            if prev:
-                weigh(s - 1, 1)
-                quantise(s - 1, 0)
-            if stt and STT_POS == 1:
-                moment_on_vector(s)
-            if len(tasks) > 1:
-                finish(*tasks[1])
-            if prev:
-                quantise(s - 1, 1)
-            if stt and STT_POS == 2:
-                moment_on_vector(s)
-            for task in tasks[2:]:
-                finish(*task)
-            if s < steps:
+                turn_x("L", g, h)
+        for g in range(G):
+            for h in range(2):
+                interleave_x("L", g, h)
+            quantise_x("L", g)
+        for g in range(G):
+            first_product(0, g)
+            tanh(0, g)
+
+        with_moment = set()
+        with_row = set()
+        waiting = sorted((max(position[("L", i)], position[("R", HALF_TILES * (h + 1) - 1)]), h, i) for h in range(2) for i in range(NJ))
+        for n in range(-1, units):
+            due = [block for block in waiting if block[0] < n and ("L", block[2]) in with_moment and block[1] in with_row][:BLOCKS_PER_STEP]
+            waiting = [block for block in waiting if block not in due]
+            for ready, h, i in due:
+                rank_one_term(i, h)
+            if n + 2 < units:
                 for g in range(G):
-                    turn_features(s, g)
-            if prev_on_act:
-                sum_p(s - 1)
+                    first_product(n + 2, g)
+                for g in range(G):
+                    tanh(n + 2, g)
+            if n >= 0:
+                weigh(n, 0)
+                weigh(n, 1)
+                quantise(n, 0)
+                if UNITS[n] in ON_SCALAR:
+                    times_p(n, 0)
+            if n + 1 < units:
+                turn_features(n + 1, 0)
+            if n >= 1 and UNITS[n - 1] in ON_SCALAR:
+                moment_on_scalar(n - 1)
+                with_moment.add(UNITS[n - 1])
+            if n + 1 < units and UNITS[n + 1] not in ON_SCALAR:
+                moment_on_vector(n + 1)
+                with_moment.add(UNITS[n + 1])
+            for ready, h, i in due:
+                finish_block(i, h)
+            if n >= 0:
+                quantise(n, 1)
+                if UNITS[n] in ON_SCALAR:
+                    times_p(n, 1)
+            if n + 1 < units:
+                turn_features(n + 1, 1)
+            if n == Z_STEP:
+                sum_of_weights()
+            for h in range(2):
+                if h not in with_row and all(("R", HALF_TILES * h + j) in with_moment for j in range(HALF_TILES)):
+                    m1_to_row(h)
+                    with_row.add(h)
+        for k, (ready, h, i) in enumerate(waiting):
+            if k == 0:
+                rank_one_term(i, h)
+            if k + 1 < len(waiting):
+                rank_one_term(waiting[k + 1][2], waiting[k + 1][1])
+            finish_block(i, h)

@@ -44,6 +44,10 @@ def tile_girsanovreweightedneurallagcovariance_d2p_kernel(tc, x0, x1_bytes, x1_s
         psum_out = ctx.enter_context(tc.psum_pool(name="psum_out", bufs=2))
         ctx.enter_context(tc.manual_schedule())
 
+        first_banks = (psum_first, "first_bank")
+        turn_banks = (psum_turn, "turn")
+        out_banks = (psum_out, "out_bank")
+
         ident = keep.tile([P, P], F32, name="ident")
         ones = keep.tile([P, P], F32, name="ones")
         minus_half = keep.tile([P, 1], F32, name="minus_half")
@@ -235,8 +239,8 @@ def tile_girsanovreweightedneurallagcovariance_d2p_kernel(tc, x0, x1_bytes, x1_s
             rank_one[(i, h)] = work.tile([P, HALF], F32, name="rank_one")
             nc.scalar.activation(rank_one[(i, h)][:], m1_row[h][:], ACT.Copy, scale=moment["L"][:, i : i + 1])
 
-        def finish_block(i, h):
-            bank = psum_out.tile([P, HALF], F32, name="out_bank")
+        def finish_block(i, h, pool, name):
+            bank = pool.tile([P, HALF], F32, name=name)
             rows = slice(P * i, P * (i + 1))
             cols = slice(HALF * h, HALF * (h + 1))
             for g in range(G):
@@ -302,8 +306,8 @@ def tile_girsanovreweightedneurallagcovariance_d2p_kernel(tc, x0, x1_bytes, x1_s
             if n + 1 < units and UNITS[n + 1] not in ON_SCALAR:
                 moment_on_vector(n + 1)
                 with_moment.add(UNITS[n + 1])
-            for ready, h, i in due:
-                finish_block(i, h)
+            for k, (ready, h, i) in enumerate(due):
+                finish_block(i, h, *(first_banks if n + 2 >= units and k == 0 else out_banks))
             if n >= 0:
                 quantise(n, 1)
                 if UNITS[n] in ON_SCALAR:
@@ -321,4 +325,4 @@ def tile_girsanovreweightedneurallagcovariance_d2p_kernel(tc, x0, x1_bytes, x1_s
                 rank_one_term(i, h)
             if k + 1 < len(waiting):
                 rank_one_term(waiting[k + 1][2], waiting[k + 1][1])
-            finish_block(i, h)
+            finish_block(i, h, *(first_banks, out_banks, turn_banks)[k % 3])

from contextlib import ExitStack

import concourse.mybir as mybir
from concourse.masks import make_identity

F32 = mybir.dt.float32
BF16 = mybir.dt.bfloat16
I32 = mybir.dt.int32
U32 = mybir.dt.uint32
U8 = mybir.dt.uint8
FP8 = mybir.dt.float8_e4m3fn
FP8X4 = mybir.dt.float8_e4m3fn_x4
FP4X4 = mybir.dt.float4_e2m1fn_x4
ALU = mybir.AluOpType
ACT = mybir.ActivationFunctionType
X_AXIS = mybir.AxisListType.X

T, D, K = 1024, 512, 1024
P = 128
R = 4
HALF = 512
G = T // HALF
NJ = K // P
HALF_TILES = HALF // P

FLOPS = 2 * (2 * T * D * K) + 2 * T * K * K

UNITS = [("R", 0), ("R", 1), ("R", 2), ("R", 3), ("L", 0), ("R", 4), ("L", 1), ("R", 5), ("L", 2), ("R", 6), ("R", 7), ("L", 3), ("L", 4), ("L", 5), ("L", 6), ("L", 7)]
ON_SCALAR = [("R", 2), ("R", 4), ("R", 5), ("R", 6), ("L", 5), ("L", 6)]
Z_STEP = 2
BLOCKS_PER_STEP = 2


def tile_girsanovreweightedneurallagcovariance_d2p_kernel(tc, x0, x1_bytes, x1_scale, w_words, w_scales, bias, a, b, out):
    nc = tc.nc
    units = len(UNITS)
    position = {unit: n for n, unit in enumerate(UNITS)}

    with ExitStack() as ctx:
        keep = ctx.enter_context(tc.tile_pool(name="keep", bufs=1))
        work = ctx.enter_context(tc.tile_pool(name="work", bufs=4))
        psum_first = ctx.enter_context(tc.psum_pool(name="psum_first", bufs=2))
        psum_turn = ctx.enter_context(tc.psum_pool(name="psum_turn", bufs=4))
        psum_out = ctx.enter_context(tc.psum_pool(name="psum_out", bufs=2))
        ctx.enter_context(tc.manual_schedule())

        first_banks = (psum_first, "first_bank")
        turn_banks = (psum_turn, "turn")
        out_banks = (psum_out, "out_bank")

        ident = keep.tile([P, P], F32, name="ident")
        ones = keep.tile([P, P], F32, name="ones")
        minus_half = keep.tile([P, 1], F32, name="minus_half")
        first_tanh = keep.tile([P, 1], F32, name="first_tanh")
        bias_square = keep.tile([P, P], F32, name="bias_square")
        bias_rows = keep.tile([NJ, P], BF16, name="bias_rows")
        bias_col = keep.tile([P, NJ], F32, name="bias_col")
        a_col = keep.tile([P, G, R], BF16, name="a_col")
        b_col = keep.tile([P, G, R], BF16, name="b_col")
        p_col = keep.tile([P, G * R], F32, name="p_col")
        p_row = keep.tile([P, G * R, P], F32, name="p_row")
        z = keep.tile([P, 1], F32, name="z")
        z_inv = keep.tile([P, 1], F32, name="z_inv")
        z_rsqrt = keep.tile([P, 1], F32, name="z_rsqrt")
        term_scale = keep.tile([P, 1], F32, name="term_scale")
        moment = {c: keep.tile([P, NJ], F32, name=f"moment{c}") for c in ("L", "R")}
        m1_row = [keep.tile([P, HALF], F32, name=f"m1_row{h}") for h in range(2)]
        x1_scales = keep.tile([P, G, R], F32, name="x1_scales")
        w_codes = keep.tile([P, 2 * K], U8, name="w_codes", align_bytes=64)
        w_planes = keep.tile([P, K], U8, name="w_planes", align_bytes=64)
        x1_in = [keep.tile([P, R, D], U8, name=f"x1_in{g}") for g in range(G)]
        x0_in = [keep.tile([P, R, D], BF16, name=f"x0_in{g}") for g in range(G)]
        pairs = {c: [keep.tile([P, R, 2, P, 2], BF16, name=f"pairs{c}{g}") for g in range(G)] for c in ("R", "L")}
        x_codes = {c: [keep.tile([P, HALF], U32, name=f"x_codes{c}{g}", align_bytes=64) for g in range(G)] for c in ("R", "L")}
        x_planes = {c: [keep.tile([P, HALF], U8, name=f"x_planes{c}{g}", align_bytes=64) for g in range(G)] for c in ("R", "L")}
        codes = {c: [keep.tile([P, K], U32, name=f"codes{c}{g}", align_bytes=64) for g in range(G)] for c in ("R", "L")}
        planes = {c: [keep.tile([P, K], U8, name=f"planes{c}{g}", align_bytes=64) for g in range(G)] for c in ("R", "L")}
        frame_weight = {"L": a_col, "R": b_col}

        x1_rows = x1_bytes.rearrange("(g p t) k -> g p t k", p=P, t=R)
        x0_rows = x0.rearrange("(g p t) k -> g p t k", p=P, t=R)
        scale_rows = x1_scale.rearrange("(g q) j -> q g j", q=4)
        for q in range(4):
            nc.scalar.dma_start(out=x1_scales[32 * q : 32 * q + 32, :, :], in_=scale_rows[q].partition_broadcast(32))
        nc.sync.dma_start(out=x1_in[0][:], in_=x1_rows[0])
        nc.sync.dma_start(out=x1_in[1][:], in_=x1_rows[1])
        nc.sync.dma_start(out=w_codes[:].bitcast(I32), in_=w_words[0].bitcast(I32))
        nc.gpsimd.memset(ones[:], 1.0)
        make_identity(nc, ident[:])
        nc.gpsimd.dma_start(out=a_col[:], in_=a.rearrange("(g p t) -> p g t", p=P, t=R))
        nc.gpsimd.dma_start(out=b_col[:], in_=b.rearrange("(g p t) -> p g t", p=P, t=R))
        nc.gpsimd.dma_start(out=bias_rows[:], in_=bias.rearrange("(j p) -> j p", p=P))
        nc.vector.memset(w_planes[:].bitcast(I32), 0)
        for q in range(4):
            nc.sync.dma_start(out=w_planes[32 * q : 32 * q + 4, :].bitcast(I32), in_=w_scales[0, 4 * q : 4 * q + 4, :].bitcast(I32))
        for g in range(G):
            nc.sync.dma_start(out=x0_in[g][:], in_=x0_rows[g])
        nc.vector.memset(first_tanh[:], 0.0)
        nc.scalar.activation(first_tanh[:], first_tanh[:], ACT.Tanh)
        nc.vector.memset(bias_square[:], 0.0)
        nc.gpsimd.memset(minus_half[:], -0.5)

        def widen_x1(g):
            for t in range(R):
                for j in range(D // P):
                    src = x1_in[g][:, t, P * j : P * (j + 1)].bitcast(FP8).rearrange("p (q u e) -> p q u e", u=2, e=2)
                    dst = pairs["R"][g][:, t, :, 32 * j : 32 * (j + 1), :].rearrange("p u q e -> p q u e")
                    nc.vector.tensor_scalar(dst, src, x1_scales[:, g, j : j + 1], None, ALU.mult)

        def sort_x0(g):
            dst = pairs["L"][g][:].rearrange("p t u q e -> p (t u q e)").bitcast(F32).rearrange("p (t u q) -> p t u q", t=R, u=2)
            src = x0_in[g][:].rearrange("p t k -> p (t k)").bitcast(F32).rearrange("p (t q u) -> p t u q", t=R, u=2)
            nc.vector.tensor_copy(out=dst, in_=src)

        turned = {}
        x_rows = {}

        def turn_x(c, g, h):
            bank = psum_turn.tile([P, 2, 2, P], F32, name="turn")
            turned[(c, g, h)] = bank
            for t in range(2):
                for u in range(2):
                    words = pairs[c][g][:, 2 * h + t, u, :, :].rearrange("p q e -> p (q e)").bitcast(F32)
                    nc.tensor.transpose(bank[:, t, u, :], words, ident[:])

        def interleave_x(c, g, h):
            if h == 0:
                x_rows[(c, g)] = work.tile([P, HALF, R], BF16, name="x_rows", align_bytes=64)
            frames = x_rows[(c, g)][:, 2 * P * h : 2 * P * (h + 1), :]
            dst = frames.rearrange("p f e -> p (f e)").bitcast(F32).rearrange("p (t f u) -> p t f u", t=2, u=2)
            nc.scalar.copy(dst, turned[(c, g, h)][:].rearrange("p t u f -> p t f u"))

        def quantise_x(c, g):
            nc.vector.quantize_mx(out=x_codes[c][g][:].bitcast(FP8X4), scales=x_planes[c][g][:], in_=x_rows[(c, g)][:].rearrange("p f e -> p (f e)"))

        def spread(bank, column, col):
            nc.tensor.transpose(bank[:, column : column + P], col.to_broadcast([P, P]), ident[:])

        def path_weights():
            nc.vector.tensor_tensor(p_col[:], a_col[:].rearrange("p g t -> p (g t)"), b_col[:].rearrange("p g t -> p (g t)"), ALU.mult)
            banks = []
            for g in range(G):
                bank = psum_turn.tile([P, HALF], F32, name="turn")
                banks.append(bank)
                for t in range(R):
                    spread(bank, P * t, p_col[:, R * g + t : R * g + t + 1])
            for g in range(G):
                nc.scalar.copy(p_row[:, R * g : R * (g + 1), :].rearrange("p c f -> p (c f)"), banks[g][:])

        def place_bias():
            nc.vector.tensor_copy(out=bias_square[0:NJ, :], in_=bias_rows[:])
            bank = psum_out.tile([P, HALF], F32, name="out_bank")
            nc.tensor.transpose(bank[:, 0:P], bias_square[:], ident[:])
            nc.scalar.copy(bias_col[:], bank[:, 0:NJ])

        def sum_of_weights():
            bank = psum_out.tile([P, HALF], F32, name="out_bank")
            nc.tensor.matmul(bank[:, 0 : G * R], ones[:], p_col[:], start=True, stop=True)
            nc.vector.tensor_reduce(z[:], bank[:, 0 : G * R], X_AXIS, ALU.add)
            nc.vector.reciprocal(z_inv[:], z[:])
            nc.gpsimd.tensor_tensor(z_rsqrt[:], z[:], minus_half[:], ALU.pow)
            nc.gpsimd.tensor_tensor(term_scale[:], z_rsqrt[:], z_inv[:], ALU.mult)
            nc.gpsimd.tensor_scalar(term_scale[:], term_scale[:], -1.0, 0.0, ALU.mult, ALU.add)

        first, features, turned_features, weighted, p_weighted = {}, {}, {}, {}, {}

        def first_product(n, g):
            c, j = UNITS[n]
            first[(n, g)] = psum_first.tile([P, HALF], F32, name="first_bank")
            nc.tensor.matmul_mx(
                out=first[(n, g)][:],
                lhsT=w_codes[:, 2 * P * j : 2 * P * (j + 1)].bitcast(FP4X4),
                lhsT_scale=w_planes[:, P * j : P * (j + 1)],
                rhs=x_codes[c][g][:].bitcast(FP8X4),
                rhs_scale=x_planes[c][g][:],
                start=True,
                stop=True,
            )

        def tanh(n, g):
            c, j = UNITS[n]
            if g == 0:
                features[n] = work.tile([P, G, HALF], F32, name="features")
            nc.scalar.activation(features[n][:, g, :], first[(n, g)][:], ACT.Tanh, bias=bias_col[:, j : j + 1])

        def turn_features(n, g):
            turned_features[(n, g)] = psum_turn.tile([P, R, P], F32, name="turn")
            for t in range(R):
                nc.tensor.transpose(turned_features[(n, g)][:, t, :], features[n][:, g, P * t : P * (t + 1)], ident[:])

        def weigh(n, g):
            c, j = UNITS[n]
            weighted[(n, g)] = work.tile([P, P, R], BF16, name="weighted", align_bytes=64)
            weights = frame_weight[c][:, g, :].unsqueeze(1).to_broadcast([P, P, R])
            nc.vector.tensor_tensor(weighted[(n, g)][:], turned_features[(n, g)][:].rearrange("p t n -> p n t"), weights, ALU.mult)

        def quantise(n, g):
            c, j = UNITS[n]
            cols = slice(P * j, P * (j + 1))
            nc.vector.quantize_mx(out=codes[c][g][:, cols].bitcast(FP8X4), scales=planes[c][g][:, cols], in_=weighted[(n, g)][:].rearrange("p n t -> p (n t)"))

        def moment_on_vector(n):
            c, j = UNITS[n]
            product = work.tile([P, T], BF16, name="product")
            nc.vector.scalar_tensor_tensor(
                out=product[:],
                in0=features[n][:].rearrange("p g f -> p (g f)"),
                scalar=1.0,
                in1=p_row[:].rearrange("p c f -> p (c f)"),
                op0=ALU.mult,
                op1=ALU.mult,
                accum_out=moment[c][:, j : j + 1],
            )

        def times_p(n, g):
            p_weighted[(n, g)] = work.tile([P, R, P], F32, name="p_weighted")
            for t in range(R):
                nc.scalar.activation(p_weighted[(n, g)][:, t, :], turned_features[(n, g)][:, t, :], ACT.Copy, scale=p_col[:, R * g + t : R * g + t + 1])

        def moment_on_scalar(n):
            c, j = UNITS[n]
            bank = psum_out.tile([P, HALF], F32, name="out_bank")
            for g in range(G):
                for t in range(R):
                    slot = R * g + t
                    nc.tensor.matmul(bank[:, 0:P], p_weighted[(n, g)][:, t, :], ident[:], start=(slot == 0), stop=(slot == G * R - 1), is_transpose=True)
            sums = work.tile([P, P], BF16, name="sums")
            nc.scalar.activation(sums[:], bank[:, 0:P], ACT.Copy, accum_out=moment[c][:, j : j + 1])

        def m1_to_row(h):
            bank = psum_out.tile([P, HALF], F32, name="out_bank")
            for j in range(HALF_TILES):
                spread(bank, P * j, moment["R"][:, HALF_TILES * h + j : HALF_TILES * h + j + 1])
            nc.scalar.activation(m1_row[h][:], bank[:], ACT.Copy, scale=term_scale[:])

        rank_one = {}

        def rank_one_term(i, h):
            rank_one[(i, h)] = work.tile([P, HALF], F32, name="rank_one")
            nc.scalar.activation(rank_one[(i, h)][:], m1_row[h][:], ACT.Copy, scale=moment["L"][:, i : i + 1])

        def finish_block(i, h, pool, name):
            bank = pool.tile([P, HALF], F32, name=name)
            rows = slice(P * i, P * (i + 1))
            cols = slice(HALF * h, HALF * (h + 1))
            for g in range(G):
                nc.tensor.matmul_mx(
                    out=bank[:],
                    lhsT=codes["L"][g][:, rows].bitcast(FP8X4),
                    lhsT_scale=planes["L"][g][:, rows],
                    rhs=codes["R"][g][:, cols].bitcast(FP8X4),
                    rhs_scale=planes["R"][g][:, cols],
                    start=(g == 0),
                    stop=(g == G - 1),
                )
            result = work.tile([P, HALF], F32, name="result", bufs=6)
            nc.vector.scalar_tensor_tensor(out=result[:], in0=bank[:], scalar=z_rsqrt[:], in1=rank_one[(i, h)][:], op0=ALU.mult, op1=ALU.add)
            nc.sync.dma_start(out=out[rows, cols], in_=result[:])

        for g in range(G):
            widen_x1(g)
        for g in range(G):
            for h in range(2):
                turn_x("R", g, h)
                interleave_x("R", g, h)
        path_weights()
        for g in range(G):
            sort_x0(g)
        place_bias()
        for g in range(G):
            quantise_x("R", g)
            for h in range(2):
                turn_x("L", g, h)
        for g in range(G):
            for h in range(2):
                interleave_x("L", g, h)
            quantise_x("L", g)
        for g in range(G):
            first_product(0, g)
            tanh(0, g)

        with_moment = set()
        with_row = set()
        waiting = sorted((max(position[("L", i)], position[("R", HALF_TILES * (h + 1) - 1)]), h, i) for h in range(2) for i in range(NJ))
        for n in range(-1, units):
            due = [block for block in waiting if block[0] < n and ("L", block[2]) in with_moment and block[1] in with_row][:BLOCKS_PER_STEP]
            waiting = [block for block in waiting if block not in due]
            for ready, h, i in due:
                rank_one_term(i, h)
            if n + 2 < units:
                for g in range(G):
                    first_product(n + 2, g)
                for g in range(G):
                    tanh(n + 2, g)
            if n >= 0:
                weigh(n, 0)
                weigh(n, 1)
                quantise(n, 0)
                if UNITS[n] in ON_SCALAR:
                    times_p(n, 0)
            if n + 1 < units:
                turn_features(n + 1, 0)
            if n >= 1 and UNITS[n - 1] in ON_SCALAR:
                moment_on_scalar(n - 1)
                with_moment.add(UNITS[n - 1])
            if n + 1 < units and UNITS[n + 1] not in ON_SCALAR:
                moment_on_vector(n + 1)
                with_moment.add(UNITS[n + 1])
            for k, (ready, h, i) in enumerate(due):
                finish_block(i, h, *(first_banks if n + 2 >= units and k == 0 else out_banks))
            if n >= 0:
                quantise(n, 1)
                if UNITS[n] in ON_SCALAR:
                    times_p(n, 1)
            if n + 1 < units:
                turn_features(n + 1, 1)
            if n == Z_STEP:
                sum_of_weights()
            for h in range(2):
                if h not in with_row and all(("R", HALF_TILES * h + j) in with_moment for j in range(HALF_TILES)):
                    m1_to_row(h)
                    with_row.add(h)
        for k, (ready, h, i) in enumerate(waiting):
            if k == 0:
                rank_one_term(i, h)
            if k + 1 < len(waiting):
                rank_one_term(waiting[k + 1][2], waiting[k + 1][1])
            finish_block(i, h, *(first_banks, out_banks, turn_banks)[k % 3])
